import numpy as np
import ml_dtypes

BF16 = ml_dtypes.bfloat16


def bf(x):
    return np.asarray(x, np.float32).astype(BF16)


def f32(x):
    return np.asarray(x, np.float32)


def f64(x):
    return np.asarray(x).astype(np.float64)


def striped(idx):
    return np.concatenate([l.reshape(-1, 16).T for l in idx])


def rows(idx, k):
    return np.tile(np.repeat(idx, 16, axis=0), (k // (16 * 8), 1))


def look(tab, idx):
    return np.take_along_axis(f64(tab), rows(idx, len(tab)), axis=1)


K, S, D, V, N = 512, 2048, 3, 512, 1536


def setup_inputs():
    return {"tab": f32(np.random.standard_normal((K, S))), "th": f32(np.random.standard_normal((K, V))), "offs": striped(np.stack([np.random.permutation(S)[:N] for _ in range(8)]))}


def reference(tab, th, offs):
    idx = np.stack([g.T.reshape(-1) for g in np.split(offs, 8)])
    x = sum((look(tab, idx[:, d * V:(d + 1) * V]) >= f64(th)) * 1.0 for d in range(D)) / D
    return x

@@ -1,0 +1,50 @@
+import concourse.mybir as mybir
+
+F32, U16 = mybir.dt.float32, mybir.dt.uint16
+IS_GE, ADD = mybir.AluOpType.is_ge, mybir.AluOpType.add
+
+P = 128
+VOTES = 3
+OFFSETS_A_COLUMN = 16
+
+FLOPS = 512 * 512 * VOTES * 2
+
+
+def tile_lookup_vote_ge_out_kernel(tc, tab, th, offs, out):
+    nc = tc.nc
+    rows, columns = tab.shape
+    width = th.shape[1]
+    blocks = rows // P
+    piece = width // OFFSETS_A_COLUMN
+
+    with (
+        tc.tile_pool(name="held", bufs=1) as held,
+        tc.tile_pool(name="loads", bufs=blocks) as loads,
+        tc.tile_pool(name="work", bufs=2) as work,
+    ):
+        offsets = held.tile([P, offs.shape[1]], U16, name="offsets")
+        nc.sync.dma_start(offsets[:], offs)
+
+        windows, thresholds = [], []
+        for b in range(blocks):
+            window = loads.tile([P, columns], F32, name="window")
+            threshold = loads.tile([P, width], F32, name="threshold")
+            nc.sync.dma_start(window[:], tab[b * P : (b + 1) * P, :])
+            nc.sync.dma_start(threshold[:], th[b * P : (b + 1) * P, :])
+            windows.append(window)
+            thresholds.append(threshold)
+
+        for b in range(blocks):
+            votes = []
+            for d in range(VOTES):
+                vote = work.tile([P, width], F32, name=f"vote{d}")
+                picked = windows[b][:].indirect(offsets[:, d * piece : (d + 1) * piece])
+                nc.vector.tensor_tensor(vote[:], picked, thresholds[b][:], IS_GE)
+                votes.append(vote)
+            pair = work.tile([P, width], F32, name="pair")
+            count = work.tile([P, width], F32, name="count")
+            share = work.tile([P, width], F32, name="share")
+            nc.vector.tensor_tensor(pair[:], votes[0][:], votes[1][:], ADD)
+            nc.vector.tensor_tensor(count[:], pair[:], votes[2][:], ADD)
+            nc.scalar.mul(share[:], count[:], 1.0 / VOTES)
+            nc.scalar.dma_start(out[b * P : (b + 1) * P, :], share[:])

@@ -1,7 +1,8 @@
 import concourse.mybir as mybir
+from concourse.masks import make_identity
 
-F32, U16 = mybir.dt.float32, mybir.dt.uint16
-IS_GE, ADD = mybir.AluOpType.is_ge, mybir.AluOpType.add
+F32, U16, BF16 = mybir.dt.float32, mybir.dt.uint16, mybir.dt.bfloat16
+IS_GE = mybir.AluOpType.is_ge
 
 P = 128
 VOTES = 3
@@ -21,9 +22,12 @@ def tile_lookup_vote_ge_out_kernel(tc, tab, th, offs, out):
         tc.tile_pool(name="held", bufs=1) as held,
         tc.tile_pool(name="loads", bufs=blocks) as loads,
         tc.tile_pool(name="work", bufs=2) as work,
+        tc.psum_pool(name="sums", bufs=2) as sums,
     ):
         offsets = held.tile([P, offs.shape[1]], U16, name="offsets")
         nc.sync.dma_start(offsets[:], offs)
+        identity = held.tile([P, P], BF16, name="identity")
+        make_identity(nc, identity[:])
 
         windows, thresholds = [], []
         for b in range(blocks):
@@ -35,16 +39,13 @@ def tile_lookup_vote_ge_out_kernel(tc, tab, th, offs, out):
             thresholds.append(threshold)
 
         for b in range(blocks):
-            votes = []
+            count = sums.tile([P, width], F32, name="count")
             for d in range(VOTES):
                 vote = work.tile([P, width], F32, name=f"vote{d}")
                 picked = windows[b][:].indirect(offsets[:, d * piece : (d + 1) * piece])
                 nc.vector.tensor_tensor(vote[:], picked, thresholds[b][:], IS_GE)
-                votes.append(vote)
-            pair = work.tile([P, width], F32, name="pair")
-            count = work.tile([P, width], F32, name="count")
+                upper_halves = vote[:].bitcast(BF16)[:, 1::2]
+                nc.tensor.matmul(count[:], identity[:], upper_halves, start=d == 0, stop=d == VOTES - 1)
             share = work.tile([P, width], F32, name="share")
-            nc.vector.tensor_tensor(pair[:], votes[0][:], votes[1][:], ADD)
-            nc.vector.tensor_tensor(count[:], pair[:], votes[2][:], ADD)
             nc.scalar.mul(share[:], count[:], 1.0 / VOTES)
             nc.scalar.dma_start(out[b * P : (b + 1) * P, :], share[:])

@@ -2,7 +2,7 @@ import concourse.mybir as mybir
 from concourse.masks import make_identity
 
 F32, U16, BF16 = mybir.dt.float32, mybir.dt.uint16, mybir.dt.bfloat16
-IS_GE = mybir.AluOpType.is_ge
+IS_GE, MULT, ADD = mybir.AluOpType.is_ge, mybir.AluOpType.mult, mybir.AluOpType.add
 
 P = 128
 VOTES = 3
@@ -39,13 +39,20 @@ def tile_lookup_vote_ge_out_kernel(tc, tab, th, offs, out):
             thresholds.append(threshold)
 
         for b in range(blocks):
+            last = b == blocks - 1
+            summed = VOTES - 1 if last else VOTES
             count = sums.tile([P, width], F32, name="count")
             for d in range(VOTES):
                 vote = work.tile([P, width], F32, name=f"vote{d}")
                 picked = windows[b][:].indirect(offsets[:, d * piece : (d + 1) * piece])
                 nc.vector.tensor_tensor(vote[:], picked, thresholds[b][:], IS_GE)
-                upper_halves = vote[:].bitcast(BF16)[:, 1::2]
-                nc.tensor.matmul(count[:], identity[:], upper_halves, start=d == 0, stop=d == VOTES - 1)
+                if d < summed:
+                    upper_halves = vote[:].bitcast(BF16)[:, 1::2]
+                    nc.tensor.matmul(count[:], identity[:], upper_halves, start=d == 0, stop=d == summed - 1)
             share = work.tile([P, width], F32, name="share")
             nc.scalar.mul(share[:], count[:], 1.0 / VOTES)
+            if last:
+                whole = work.tile([P, width], F32, name="whole")
+                nc.vector.scalar_tensor_tensor(whole[:], vote[:], 1.0 / VOTES, share[:], MULT, ADD)
+                share = whole
             nc.scalar.dma_start(out[b * P : (b + 1) * P, :], share[:])

import concourse.mybir as mybir
from concourse.masks import make_identity

F32, U16, BF16 = mybir.dt.float32, mybir.dt.uint16, mybir.dt.bfloat16
IS_GE, MULT, ADD = mybir.AluOpType.is_ge, mybir.AluOpType.mult, mybir.AluOpType.add

P = 128
VOTES = 3
OFFSETS_A_COLUMN = 16

FLOPS = 512 * 512 * VOTES * 2


def tile_lookup_vote_ge_out_kernel(tc, tab, th, offs, out):
    nc = tc.nc
    rows, columns = tab.shape
    width = th.shape[1]
    blocks = rows // P
    piece = width // OFFSETS_A_COLUMN

    with (
        tc.tile_pool(name="held", bufs=1) as held,
        tc.tile_pool(name="loads", bufs=blocks) as loads,
        tc.tile_pool(name="work", bufs=2) as work,
        tc.psum_pool(name="sums", bufs=2) as sums,
    ):
        offsets = held.tile([P, offs.shape[1]], U16, name="offsets")
        nc.sync.dma_start(offsets[:], offs)
        identity = held.tile([P, P], BF16, name="identity")
        make_identity(nc, identity[:])

        windows, thresholds = [], []
        for b in range(blocks):
            window = loads.tile([P, columns], F32, name="window")
            threshold = loads.tile([P, width], F32, name="threshold")
            nc.sync.dma_start(window[:], tab[b * P : (b + 1) * P, :])
            nc.sync.dma_start(threshold[:], th[b * P : (b + 1) * P, :])
            windows.append(window)
            thresholds.append(threshold)

        for b in range(blocks):
            last = b == blocks - 1
            summed = VOTES - 1 if last else VOTES
            count = sums.tile([P, width], F32, name="count")
            for d in range(VOTES):
                vote = work.tile([P, width], F32, name=f"vote{d}")
                picked = windows[b][:].indirect(offsets[:, d * piece : (d + 1) * piece])
                nc.vector.tensor_tensor(vote[:], picked, thresholds[b][:], IS_GE)
                if d < summed:
                    upper_halves = vote[:].bitcast(BF16)[:, 1::2]
                    nc.tensor.matmul(count[:], identity[:], upper_halves, start=d == 0, stop=d == summed - 1)
            share = work.tile([P, width], F32, name="share")
            nc.scalar.mul(share[:], count[:], 1.0 / VOTES)
            if last:
                whole = work.tile([P, width], F32, name="whole")
                nc.vector.scalar_tensor_tensor(whole[:], vote[:], 1.0 / VOTES, share[:], MULT, ADD)
                share = whole
            nc.scalar.dma_start(out[b * P : (b + 1) * P, :], share[:])
